import numpy as np
import ml_dtypes

BF16 = ml_dtypes.bfloat16


def bf(x):
    return np.asarray(x, np.float32).astype(BF16)


def f32(x):
    return np.asarray(x, np.float32)


def f64(x):
    return np.asarray(x).astype(np.float64)


def striped(idx):
    return np.tile(idx.reshape(-1, 16).T, (8, 1))


S, K, N, V, F, H, O = 2048, 128, 512, 256, 2, 128, 128


def gelu_tanh(v):
    return 0.5 * v * (1.0 + np.tanh(np.sqrt(2.0 / np.pi) * (v + 0.044715 * v**3)))


def setup_inputs():
    return {"table": bf(np.random.standard_normal((F, K, S))), "w": bf(np.random.standard_normal((F, K, H)) / np.sqrt(F * K)), "b": f32(0.5 * np.random.standard_normal((H, 1))), "w2": bf(np.random.standard_normal((H, O)) / np.sqrt(H)), "b2": f32(0.5 * np.random.standard_normal((O, 1))), "offs": striped(np.concatenate([np.random.permutation(np.tile(np.arange(S), 2))[:V] for _ in range(F)]))}


def reference(table, w, b, w2, b2, offs):
    idx = offs[:16].T.reshape(-1)
    t = sum(f64(w)[f].T @ f64(table)[f][:, idx[f * V : (f + 1) * V]] for f in range(F)) + f64(b)
    t = gelu_tanh(t)
    return f64(w2).T @ t + f64(b2)

import concourse.mybir as mybir

FIELDS, FEATURES, VALUES, SAMPLES, HIDDEN, OUTPUTS = 2, 128, 2048, 256, 128, 128
FLOPS = 2 * SAMPLES * HIDDEN * (FIELDS * FEATURES + OUTPUTS)

BF16, F32, U16 = mybir.dt.bfloat16, mybir.dt.float32, mybir.dt.uint16
GELU = mybir.ActivationFunctionType.Gelu_apprx_tanh
ADD = mybir.AluOpType.add

ENTRIES_PER_COLUMN = 16
COLUMNS_PER_FIELD = SAMPLES // ENTRIES_PER_COLUMN


def tile_rows_fields2_gelu_kernel(tc, table, w, b, w2, b2, offs, out):
    nc = tc.nc
    with (
        tc.tile_pool(name="held", bufs=1) as held,
        tc.psum_pool(name="psum", bufs=1) as psum,
    ):
        offsets = held.tile([128, FIELDS * COLUMNS_PER_FIELD], U16, name="offsets")
        windows = [held.tile([FEATURES, VALUES], BF16, name=f"window{f}") for f in range(FIELDS)]
        layer1 = held.tile([FEATURES, FIELDS, HIDDEN], BF16, name="layer1")
        layer2 = held.tile([HIDDEN, OUTPUTS], BF16, name="layer2")
        bias1 = held.tile([HIDDEN, 1], F32, name="bias1")
        bias2 = held.tile([OUTPUTS, 1], F32, name="bias2")

        nc.sync.dma_start(windows[0][:], table[0])
        nc.sync.dma_start(offsets[:], offs)
        nc.sync.dma_start(windows[1][:], table[1])
        nc.sync.dma_start(layer2[:], w2)
        nc.sync.dma_start(bias2[:], b2)
        nc.scalar.dma_start(layer1[:], w.rearrange("f k h -> k f h"))
        nc.scalar.dma_start(bias1[:], b)

        summed = psum.tile([HIDDEN, SAMPLES], F32, name="summed")
        for f in range(FIELDS):
            picks = offsets[:, f * COLUMNS_PER_FIELD : (f + 1) * COLUMNS_PER_FIELD]
            nc.tensor.matmul(
                summed[:], layer1[:, f, :], windows[f][:].indirect(picks), start=(f == 0), stop=(f == FIELDS - 1)
            )
        hidden = held.tile([HIDDEN, SAMPLES], BF16, name="hidden")
        nc.scalar.activation(hidden[:], summed[:], GELU, bias=bias1[:])

        product = psum.tile([OUTPUTS, SAMPLES], F32, name="product")
        nc.tensor.matmul(product[:], layer2[:], hidden[:], start=True, stop=True)
        result = held.tile([OUTPUTS, SAMPLES], F32, name="result")
        nc.vector.tensor_scalar(result[:], product[:], bias2[:], None, ADD)
        nc.sync.dma_start(out, result[:])
